import numpy as np
import ml_dtypes


def mxq(x, axis, fmt="e4m3"):
    dtype, down = {"e4m3": (ml_dtypes.float8_e4m3fn, 7), "e5m2": (ml_dtypes.float8_e5m2, 14)}[fmt]
    v = np.moveaxis(np.asarray(x, np.float32).astype(ml_dtypes.bfloat16).astype(np.float64), axis, -1)
    blocks = v.reshape(v.shape[:-1] + (-1, 32))
    amax = np.abs(blocks).max(-1, keepdims=True)
    byte = np.maximum(np.where(amax > 0, np.frexp(amax)[1] - 1 + 127, 0) - down, 1)
    scale = np.exp2(byte - 127.0)
    codes = (blocks / scale).astype(np.float32).astype(dtype).astype(np.float64)
    return np.moveaxis((codes * scale).reshape(v.shape), -1, axis)


WIDE = False


def mx_kscale(k):
    if not WIDE:
        return np.ones(k)
    levels = np.array([10, -10, 5, -5, 0])
    if k % 512:
        return np.exp2(np.random.permutation(np.resize(levels, k // 32))).repeat(32)
    a = np.empty((k // 512, 16))
    for p in range(k // 512):
        a[p, :8] = np.random.permutation(np.resize(levels, 8))
        for g in range(8):
            far = levels[np.abs(levels - a[p, g]) >= 10]
            a[p, g + 8] = far[np.random.randint(len(far))]
    return np.exp2(a.ravel()).repeat(32)


BF16 = ml_dtypes.bfloat16


def bf(x):
    return np.asarray(x, np.float32).astype(BF16)


def f64(x):
    return np.asarray(x).astype(np.float64)

def planes(Y):
    n, m = Y.shape
    b = f64(bf(Y)).reshape(n // 32, 32, m)
    amax = np.abs(b).max(1)
    byte = np.clip(np.where(amax > 0, np.frexp(amax)[1] - 1 + 127 - 7, 1), 1, 254)
    codes = (b * np.exp2(127.0 - byte)[:, None, :]).reshape(n, m).astype(np.float32).astype(ml_dtypes.float8_e4m3fn).view(np.uint8)
    words = codes.reshape(n // 512, 128, 4, m).transpose(0, 1, 3, 2)
    return np.ascontiguousarray(words), np.ascontiguousarray(byte.astype(np.uint8).reshape(n // 512, 16, m))


T, D, F = 512, 1536, 1024


def setup_inputs():
    s = mx_kscale(F)
    u = mx_kscale(D)
    t = mx_kscale(D)
    g = np.exp(0.8 * np.random.randn(F))
    mom = np.random.randn(D, F) * D ** -0.25
    pre_out = np.random.randn(F, F) / np.sqrt(F) * g[None, :]
    damp = 0.5 * g * np.exp(0.2 * np.random.randn(F))
    pre_in = np.random.randn(D, D) / np.sqrt(D)
    lr = 0.8 * D ** -0.25 * np.exp(0.3 * np.random.randn(D))
    xt = np.random.randn(D, T)
    base = 0.7 * np.random.randn(T, F) * g[None, :]
    return {
        "mom": bf(mom * t[:, None] * s[None, :]),
        "pre_out": bf(pre_out / s[:, None]),
        "damp": bf(damp / s),
        "pre_in": bf(pre_in / u[None, :]),
        "lr": bf(lr / t),
        "xt": bf(xt * u[:, None]),
        "base": bf(base),
    }

def reference(mom, pre_out, damp, pre_in, lr, xt, base):
    mom, pre_out, damp, pre_in = f64(mom), f64(pre_out), f64(damp), f64(pre_in)
    lr, xt, base = f64(lr), f64(xt), f64(base)
    a = (mxq(mom, 1, "e4m3") @ mxq(pre_out, 0, "e4m3")) + damp[None, :] * mom
    z = lr[:, None] * (mxq(pre_in, 1, "e4m3") @ mxq(xt, 0, "e4m3"))
    y = base - (mxq(z, 0, "e4m3").T @ mxq(a, 0, "e4m3"))
    Y = y.T
    words, scales = planes(Y)
    return y, words, scales

@@ -1,0 +1,382 @@
+from contextlib import ExitStack
+
+import concourse.mybir as mybir
+from concourse.masks import make_identity
+
+T, D, F = 512, 1536, 1024
+FLOPS = 2 * D * F * F + 2 * D * D * T + 2 * T * D * F
+
+F32 = mybir.dt.float32
+BF16 = mybir.dt.bfloat16
+U32 = mybir.dt.uint32
+I32 = mybir.dt.int32
+U8 = mybir.dt.uint8
+FP8X4 = mybir.dt.float8_e4m3fn_x4
+MULT = mybir.AluOpType.mult
+ADD = mybir.AluOpType.add
+SUBTRACT = mybir.AluOpType.subtract
+
+P = 128
+PASS = 512
+D_GROUPS = D // PASS
+F_GROUPS = F // PASS
+S_TILES = T // P
+LOAD_SLOTS = 16
+ALIGN = 64
+
+
+def tile_preconditioned_momentum_outputs_h3_kernel(
+    tc, mom, pre_out, damp, pre_in, lr, xt, base, out_0, out_1, out_2
+):
+    nc = tc.nc
+    with ExitStack() as ctx:
+        keep = ctx.enter_context(tc.tile_pool(name="keep", bufs=1))
+        psum = ctx.enter_context(tc.psum_pool(name="psum", bufs=1))
+        ctx.enter_context(tc.manual_schedule())
+
+        taken = {}
+
+        def rotating(pool, tag, slots, shape, dtype):
+            turn = taken.get(tag, 0)
+            taken[tag] = turn + 1
+            name = "%s%d" % (tag, turn % slots)
+            if pool == "psum":
+                return psum.tile(shape, dtype, name=name, tag=name)
+            return keep.tile(shape, dtype, name=name, tag=name, align_bytes=ALIGN)
+
+        def operand(name):
+            codes = keep.tile([P, PASS], U32, name=name + "_codes", align_bytes=ALIGN)
+            scales = keep.tile([P, PASS], U8, name=name + "_scales", align_bytes=ALIGN)
+            return codes, scales
+
+        def quantize(q, grouped, c0=0, width=PASS):
+            nc.vector.quantize_mx(
+                out=q[0][:, c0 : c0 + width].bitcast(FP8X4),
+                scales=q[1][:, c0 : c0 + width],
+                in_=grouped,
+            )
+
+        def matmul(acc, stat, s0, mov, m0, width, start, stop):
+            nc.tensor.matmul_mx(
+                out=acc,
+                lhsT=stat[0][:, s0 : s0 + P].bitcast(FP8X4),
+                lhsT_scale=stat[1][:, s0 : s0 + P],
+                rhs=mov[0][:, m0 : m0 + width].bitcast(FP8X4),
+                rhs_scale=mov[1][:, m0 : m0 + width],
+                start=start,
+                stop=stop,
+            )
+
+        raw = {}
+
+        def load(key, src):
+            raw[key] = rotating("sbuf", "raw", LOAD_SLOTS, list(src.shape), BF16)
+            nc.sync.dma_start(out=raw[key][:], in_=src)
+
+        def load_mom(g, u):
+            rows = mom[PASS * g : PASS * (g + 1), :].rearrange("(m t) k -> m t k", t=4)
+            load(("mom", g, u), rows[:, 2 * u : 2 * u + 2, :])
+
+        def load_pre_out(kk, h):
+            rows = pre_out[PASS * kk : PASS * (kk + 1), PASS * h : PASS * (h + 1)]
+            load(("pre_out", kk, h), rows.rearrange("(p j) c -> p j c", j=4))
+
+        def load_pre_in(g, kk):
+            rows = pre_in[PASS * g : PASS * (g + 1), PASS * kk : PASS * (kk + 1)]
+            load(("pre_in", g, kk), rows.rearrange("(m t) k -> m t k", t=4))
+
+        def load_xt(kk):
+            load(("xt", kk), xt[PASS * kk : PASS * (kk + 1), :].rearrange("(p j) s -> p j s", j=4))
+
+        def load_base(i):
+            load(("base", i), base[2 * P * i : 2 * P * (i + 1), :].rearrange("(a p) f -> p a f", p=P))
+
+        ident = keep.tile([P, P], F32, name="ident")
+        damp_sb = keep.tile([P, F_GROUPS, 4], BF16, name="damp_sb")
+        lr_sb = keep.tile([P, D_GROUPS, 4], BF16, name="lr_sb")
+        mom_t = {}
+        mom_q, pre_out_q, pre_in_q, xt_q, a_q, z_q = {}, {}, {}, {}, {}, {}
+        for g in range(D_GROUPS):
+            z_q[g] = operand("z%d" % g)
+            xt_q[g] = operand("xt%d" % g)
+            for kk in range(D_GROUPS):
+                pre_in_q[g, kk] = operand("pre_in%d%d" % (g, kk))
+            for h in range(F_GROUPS):
+                mom_q[g, h] = operand("mom%d%d" % (g, h))
+                a_q[g, h] = operand("a%d%d" % (g, h))
+                mom_t[g, h] = keep.tile([P, PASS * 4], BF16, name="mom_t%d%d" % (g, h), align_bytes=ALIGN)
+        for kk in range(F_GROUPS):
+            for h in range(F_GROUPS):
+                pre_out_q[kk, h] = operand("pre_out%d%d" % (kk, h))
+        y_codes = [keep.tile([P, F_GROUPS, P], U32, name="y_codes%d" % st, align_bytes=ALIGN) for st in range(S_TILES)]
+        y_scales = keep.tile([P, F_GROUPS, T], U8, name="y_scales", align_bytes=ALIGN)
+        grouped = {}
+
+        def copy_on(engine, out, in_):
+            if engine == "vector":
+                nc.vector.tensor_copy(out=out, in_=in_)
+            else:
+                nc.scalar.copy(out=out, in_=in_)
+
+        def stage(key):
+            if key not in grouped:
+                grouped[key] = rotating("sbuf", "grouped", 5, [P, PASS * 4], BF16)
+            return grouped[key]
+
+        def weave_pre_out(engine, kk, h, half):
+            key = ("pre_out", kk, h)
+            dst = stage(key)[:].rearrange("p (t m j) -> p t m j", t=4, j=4)
+            src = raw[key][:].rearrange("p j (m t) -> p t m j", t=4)
+            copy_on(engine, dst[:, 2 * half : 2 * half + 2], src[:, 2 * half : 2 * half + 2])
+
+        def weave_xt(engine, kk, half):
+            key = ("xt", kk)
+            dst = stage(key)[:].rearrange("p (c i j) -> p c j i", i=4, j=4)
+            src = raw[key][:].rearrange("p j (c i) -> p c j i", i=4)
+            copy_on(engine, dst[:, 64 * half : 64 * (half + 1)], src[:, 64 * half : 64 * (half + 1)])
+
+        def turn_mom(g, u):
+            words = raw["mom", g, u][:].bitcast(F32)
+            for kk in range(F_GROUPS):
+                bank = rotating("psum", "turn", 4, [P, 2, 2, P], F32)
+                for e in range(2):
+                    for w in range(2):
+                        nc.tensor.transpose(
+                            bank[:, e, w, :], words[:, e, 256 * kk + w : 256 * (kk + 1) : 2], ident[:]
+                        )
+                dst = mom_t[g, kk][:].bitcast(F32).rearrange("p (u m e w) -> p u m e w", u=2, e=2, w=2)
+                nc.scalar.copy(out=dst[:, u], in_=bank[:].rearrange("p e w m -> p m e w"))
+
+        def turn_pre_in(g, kk):
+            key = ("pre_in", g, kk)
+            words = raw[key][:].bitcast(F32)
+            dst = stage(key)[:].bitcast(F32).rearrange("p (t m w) -> p t m w", t=4, w=2)
+            for v in range(2):
+                bank = rotating("psum", "turn", 4, [P, 2, 2, P], F32)
+                for e in range(2):
+                    for w in range(2):
+                        nc.tensor.transpose(bank[:, e, w, :], words[:, 2 * v + e, w:256:2], ident[:])
+                nc.scalar.copy(out=dst[:, 2 * v : 2 * v + 2], in_=bank[:].rearrange("p e w m -> p e m w"))
+            quantize(pre_in_q[g, kk], grouped[key][:])
+
+        def warm_up(passes):
+            bank = rotating("psum", "acc", 4, [P, PASS], F32)
+            for i in range(passes):
+                matmul(bank[:], pre_out_q[0, 0], 0, pre_out_q[0, 0], 0, PASS, True, True)
+
+        a_t = {}
+
+        def product_a(g, h):
+            a_t[g, h] = rotating("sbuf", "a_t", 4, [P, 4, PASS], BF16)
+            mom_cols = mom_t[g, h][:].rearrange("p (c t) -> p t c", t=4)
+            for t in range(4):
+                bank = rotating("psum", "acc", 4, [P, PASS], F32)
+                for kk in range(F_GROUPS):
+                    matmul(bank[:], pre_out_q[kk, h], P * t, mom_q[g, kk], 0, PASS, kk == 0, kk == F_GROUPS - 1)
+                nc.vector.scalar_tensor_tensor(
+                    out=a_t[g, h][:, t, :],
+                    in0=mom_cols[:, t, :],
+                    scalar=damp_sb[:, h, t : t + 1],
+                    in1=bank[:],
+                    op0=MULT,
+                    op1=ADD,
+                )
+
+        def turn_a(g, h):
+            key = ("a", g, h)
+            words = a_t[g, h][:].bitcast(F32)
+            dst = stage(key)[:].bitcast(F32).rearrange("p (t m u) -> p t m u", t=4, u=2)
+            for v in range(2):
+                bank = rotating("psum", "turn", 4, [P, 2, 2, P], F32)
+                for e in range(2):
+                    for u in range(2):
+                        nc.tensor.transpose(bank[:, e, u, :], words[:, 2 * v + e, P * u : P * (u + 1)], ident[:])
+                nc.scalar.copy(out=dst[:, 2 * v : 2 * v + 2], in_=bank[:].rearrange("p e u m -> p e m u"))
+            quantize(a_q[g, h], grouped[key][:])
+
+        z_b = {}
+
+        def product_z(g, st):
+            bank = rotating("psum", "acc", 4, [P, 4, P], F32)
+            for t in range(4):
+                for kk in range(D_GROUPS):
+                    matmul(bank[:, t, :], pre_in_q[g, kk], P * t, xt_q[kk], P * st, P, kk == 0, kk == D_GROUPS - 1)
+            z_b[g, st] = rotating("sbuf", "z_b", 3, [P, P * 4], BF16)
+            nc.vector.tensor_tensor(
+                out=z_b[g, st][:].rearrange("p (s t) -> p s t", t=4),
+                in0=bank[:].rearrange("p t s -> p s t"),
+                in1=lr_sb[:, g, :].unsqueeze(1).to_broadcast([P, P, 4]),
+                op=MULT,
+            )
+
+        def quantize_z(g, st):
+            quantize(z_q[g], z_b[g, st][:], P * st, P)
+
+        y_b = {}
+
+        def product_y(st, h):
+            bank = rotating("psum", "acc", 4, [P, PASS], F32)
+            for g in range(D_GROUPS):
+                matmul(bank[:], z_q[g], P * st, a_q[g, h], 0, PASS, g == 0, g == D_GROUPS - 1)
+            y = rotating("sbuf", "y", 6, [P, PASS], F32)
+            cols = slice(PASS * h, PASS * (h + 1))
+            nc.vector.tensor_tensor(
+                out=y[:].rearrange("p (m t) -> p m t", t=4),
+                in0=raw["base", st // 2][:, st % 2, cols].rearrange("p (m t) -> p m t", t=4),
+                in1=bank[:].rearrange("p (t m) -> p m t", t=4),
+                op=SUBTRACT,
+            )
+            y_b[st, h] = rotating("sbuf", "y_b", 4, [P, PASS], BF16)
+            nc.scalar.copy(
+                out=y_b[st, h][:].rearrange("p (u m e) -> p u m e", u=2, e=2),
+                in_=y[:].rearrange("p (m u e) -> p u m e", u=2, e=2),
+            )
+            nc.sync.dma_start(out=out_0[P * st : P * (st + 1), cols], in_=y[:])
+
+        y_g = {}
+
+        def turn_y(st, h):
+            words = y_b[st, h][:].bitcast(F32)
+            bank = rotating("psum", "turn", 4, [P, 2, P], F32)
+            for u in range(2):
+                nc.tensor.transpose(bank[:, u, :], words[:, P * u : P * (u + 1)], ident[:])
+            y_g[st, h] = rotating("sbuf", "y_g", 4, [P, P * 4], BF16)
+            nc.scalar.copy(
+                out=y_g[st, h][:].bitcast(F32).rearrange("p (s u) -> p s u", u=2),
+                in_=bank[:].rearrange("p u s -> p s u"),
+            )
+
+        def quantize_y(st, h):
+            quantize((y_codes[st][:, h, :], y_scales[:, h, P * st : P * (st + 1)]), y_g[st, h][:], 0, P)
+
+        def store_words(st):
+            cols = slice(P * st, P * (st + 1))
+            words = out_1.rearrange("h p s b -> p h (s b)").bitcast(I32)
+            nc.sync.dma_start(out=words[:, :, cols], in_=y_codes[st][:].bitcast(I32))
+
+        def store_scales():
+            for q in range(4):
+                queue = nc.scalar if q % 2 else nc.sync
+                queue.dma_start(
+                    out=out_2[:, 4 * q : 4 * q + 4, :].rearrange("h r s -> r h s").bitcast(I32),
+                    in_=y_scales[32 * q : 32 * q + 4].bitcast(I32),
+                )
+
+
+        make_identity(nc, ident[:])
+        load_mom(0, 0)
+        load_pre_out(0, 0)
+        load_mom(0, 1)
+        load_pre_out(1, 0)
+        load_mom(1, 0)
+        load_mom(1, 1)
+        load_pre_out(0, 1)
+        load_mom(2, 0)
+        with nc.allow_non_contiguous_dma(reason="one short run of a vector to each partition"):
+            nc.sync.dma_start(out=damp_sb[:], in_=damp.rearrange("(h p t) -> p h t", p=P, t=4))
+        load_mom(2, 1)
+        load_pre_in(0, 0)
+        load_pre_out(1, 1)
+        load_pre_in(0, 1)
+        load_pre_in(0, 2)
+        for kk in range(3):
+            load_xt(kk)
+
+        turn_mom(0, 0)
+        weave_pre_out("vector", 0, 0, 0)
+        weave_pre_out("vector", 0, 0, 1)
+        turn_mom(0, 1)
+        quantize(pre_out_q[0, 0], grouped["pre_out", 0, 0][:])
+        weave_pre_out("vector", 1, 0, 0)
+        weave_pre_out("scalar", 1, 0, 1)
+        quantize(mom_q[0, 0], mom_t[0, 0][:])
+        quantize(mom_q[0, 1], mom_t[0, 1][:])
+        quantize(pre_out_q[1, 0], grouped["pre_out", 1, 0][:])
+        warm_up(2)
+        turn_mom(1, 0)
+        with nc.allow_non_contiguous_dma(reason="one short run of a vector to each partition"):
+            nc.sync.dma_start(out=lr_sb[:], in_=lr.rearrange("(g p t) -> p g t", p=P, t=4))
+        for kk in range(3):
+            load_pre_in(1, kk)
+        warm_up(2)
+        turn_mom(1, 1)
+        quantize(mom_q[1, 0], mom_t[1, 0][:])
+        quantize(mom_q[1, 1], mom_t[1, 1][:])
+        weave_pre_out("scalar", 0, 1, 0)
+        weave_pre_out("scalar", 0, 1, 1)
+        product_a(0, 0)
+        turn_mom(2, 0)
+        turn_mom(2, 1)
+        for kk in range(3):
+            load_pre_in(2, kk)
+        quantize(pre_out_q[0, 1], grouped["pre_out", 0, 1][:])
+        weave_pre_out("scalar", 1, 1, 0)
+        weave_pre_out("scalar", 1, 1, 1)
+        quantize(mom_q[2, 0], mom_t[2, 0][:])
+        quantize(mom_q[2, 1], mom_t[2, 1][:])
+        product_a(1, 0)
+        turn_pre_in(0, 0)
+        load_base(0)
+        load_base(1)
+        weave_xt("scalar", 0, 0)
+        weave_xt("scalar", 0, 1)
+        quantize(pre_out_q[1, 1], grouped["pre_out", 1, 1][:])
+        product_a(2, 0)
+        turn_pre_in(0, 1)
+        turn_pre_in(0, 2)
+        quantize(xt_q[0], grouped["xt", 0][:])
+        weave_xt("scalar", 1, 0)
+        weave_xt("scalar", 1, 1)
+        product_a(0, 1)
+        turn_a(0, 0)
+        turn_pre_in(1, 0)
+        quantize(xt_q[1], grouped["xt", 1][:])
+        weave_xt("scalar", 2, 0)
+        weave_xt("scalar", 2, 1)
+        product_a(1, 1)
+        turn_a(1, 0)
+        turn_pre_in(1, 1)
+        quantize(xt_q[2], grouped["xt", 2][:])
+        product_a(2, 1)
+        turn_a(2, 0)
+        turn_pre_in(1, 2)
+        for st in range(4):
+            product_z(0, st)
+            if st > 0:
+                quantize_z(0, st - 1)
+        turn_pre_in(2, 0)
+        quantize_z(0, 3)
+        turn_a(0, 1)
+        product_z(1, 0)
+        product_z(1, 1)
+        quantize_z(1, 0)
+        turn_pre_in(2, 1)
+        quantize_z(1, 1)
+        turn_pre_in(2, 2)
+        product_z(1, 2)
+        product_z(1, 3)
+        quantize_z(1, 2)
+        turn_a(1, 1)
+        quantize_z(1, 3)
+        turn_a(2, 1)
+        product_z(2, 0)
+        product_z(2, 1)
+        quantize_z(2, 0)
+        product_z(2, 2)
+        quantize_z(2, 1)
+        product_y(0, 0)
+        quantize_z(2, 2)
+        product_z(2, 3)
+        product_y(0, 1)
+        quantize_z(2, 3)
+        product_y(1, 0)
+        product_y(1, 1)
+        for st in range(2, 6):
+            for h in range(2):
+                turn_y(st - 2, h)
+            for h in range(2):
+                if st < 4:
+                    product_y(st, h)
+                quantize_y(st - 2, h)
+            store_words(st - 2)
+        store_scales()

@@ -15,6 +15,7 @@ FP8X4 = mybir.dt.float8_e4m3fn_x4
 MULT = mybir.AluOpType.mult
 ADD = mybir.AluOpType.add
 SUBTRACT = mybir.AluOpType.subtract
+COPY = mybir.ActivationFunctionType.Copy
 
 P = 128
 PASS = 512
@@ -73,9 +74,9 @@ def tile_preconditioned_momentum_outputs_h3_kernel(
             raw[key] = rotating("sbuf", "raw", LOAD_SLOTS, list(src.shape), BF16)
             nc.sync.dma_start(out=raw[key][:], in_=src)
 
-        def load_mom(g, u):
-            rows = mom[PASS * g : PASS * (g + 1), :].rearrange("(m t) k -> m t k", t=4)
-            load(("mom", g, u), rows[:, 2 * u : 2 * u + 2, :])
+        def load_mom(g, kk):
+            rows = mom[PASS * g : PASS * (g + 1), PASS * kk : PASS * (kk + 1)]
+            load(("mom", g, kk), rows.rearrange("(m t) k -> m t k", t=4))
 
         def load_pre_out(kk, h):
             rows = pre_out[PASS * kk : PASS * (kk + 1), PASS * h : PASS * (h + 1)]
@@ -94,6 +95,7 @@ def tile_preconditioned_momentum_outputs_h3_kernel(
         ident = keep.tile([P, P], F32, name="ident")
         damp_sb = keep.tile([P, F_GROUPS, 4], BF16, name="damp_sb")
         lr_sb = keep.tile([P, D_GROUPS, 4], BF16, name="lr_sb")
+        lr_f = keep.tile([P, D_GROUPS, 4], F32, name="lr_f")
         mom_t = {}
         mom_q, pre_out_q, pre_in_q, xt_q, a_q, z_q = {}, {}, {}, {}, {}, {}
         for g in range(D_GROUPS):
@@ -108,7 +110,6 @@ def tile_preconditioned_momentum_outputs_h3_kernel(
         for kk in range(F_GROUPS):
             for h in range(F_GROUPS):
                 pre_out_q[kk, h] = operand("pre_out%d%d" % (kk, h))
-        y_codes = [keep.tile([P, F_GROUPS, P], U32, name="y_codes%d" % st, align_bytes=ALIGN) for st in range(S_TILES)]
         y_scales = keep.tile([P, F_GROUPS, T], U8, name="y_scales", align_bytes=ALIGN)
         grouped = {}
 
@@ -120,14 +121,14 @@ def tile_preconditioned_momentum_outputs_h3_kernel(
 
         def stage(key):
             if key not in grouped:
-                grouped[key] = rotating("sbuf", "grouped", 5, [P, PASS * 4], BF16)
+                grouped[key] = rotating("sbuf", "grouped", 6, [P, PASS * 4], BF16)
             return grouped[key]
 
-        def weave_pre_out(engine, kk, h, half):
+        def weave_pre_out(engine, kk, h, t0, t1):
             key = ("pre_out", kk, h)
             dst = stage(key)[:].rearrange("p (t m j) -> p t m j", t=4, j=4)
             src = raw[key][:].rearrange("p j (m t) -> p t m j", t=4)
-            copy_on(engine, dst[:, 2 * half : 2 * half + 2], src[:, 2 * half : 2 * half + 2])
+            copy_on(engine, dst[:, t0:t1], src[:, t0:t1])
 
         def weave_xt(engine, kk, half):
             key = ("xt", kk)
@@ -135,52 +136,70 @@ def tile_preconditioned_momentum_outputs_h3_kernel(
             src = raw[key][:].rearrange("p j (c i) -> p c j i", i=4)
             copy_on(engine, dst[:, 64 * half : 64 * (half + 1)], src[:, 64 * half : 64 * (half + 1)])
 
-        def turn_mom(g, u):
-            words = raw["mom", g, u][:].bitcast(F32)
-            for kk in range(F_GROUPS):
+        def turn_mom(g, kk):
+            words = raw["mom", g, kk][:].bitcast(F32)
+            dst = mom_t[g, kk][:].bitcast(F32).rearrange("p (u m e w) -> p u m e w", u=2, e=2, w=2)
+            for u in range(2):
                 bank = rotating("psum", "turn", 4, [P, 2, 2, P], F32)
                 for e in range(2):
                     for w in range(2):
-                        nc.tensor.transpose(
-                            bank[:, e, w, :], words[:, e, 256 * kk + w : 256 * (kk + 1) : 2], ident[:]
-                        )
-                dst = mom_t[g, kk][:].bitcast(F32).rearrange("p (u m e w) -> p u m e w", u=2, e=2, w=2)
+                        nc.tensor.transpose(bank[:, e, w, :], words[:, 2 * u + e, w:256:2], ident[:])
                 nc.scalar.copy(out=dst[:, u], in_=bank[:].rearrange("p e w m -> p m e w"))
+
+        halves = {}
+
+        def sort_pre_in(engine, g, kk):
+            key = ("pre_in", g, kk)
+            halves[key] = rotating("sbuf", "raw", LOAD_SLOTS, [P, 4, 2, P], F32)
+            src = raw[key][:].bitcast(F32).rearrange("p t (c i w) -> p t c w i", i=4, w=2)
+            copy_on(engine, halves[key][:].rearrange("p t w (c i) -> p t c w i", i=4), src)
 
         def turn_pre_in(g, kk):
             key = ("pre_in", g, kk)
-            words = raw[key][:].bitcast(F32)
+            if key in halves:
+                words = halves[key]
+            else:
+                words = raw[key][:].bitcast(F32).rearrange("p t (m w) -> p t w m", w=2)
             dst = stage(key)[:].bitcast(F32).rearrange("p (t m w) -> p t m w", t=4, w=2)
             for v in range(2):
                 bank = rotating("psum", "turn", 4, [P, 2, 2, P], F32)
                 for e in range(2):
                     for w in range(2):
-                        nc.tensor.transpose(bank[:, e, w, :], words[:, 2 * v + e, w:256:2], ident[:])
+                        nc.tensor.transpose(bank[:, e, w, :], words[:, 2 * v + e, w, :], ident[:])
                 nc.scalar.copy(out=dst[:, 2 * v : 2 * v + 2], in_=bank[:].rearrange("p e w m -> p e m w"))
             quantize(pre_in_q[g, kk], grouped[key][:])
 
-        def warm_up(passes):
-            bank = rotating("psum", "acc", 4, [P, PASS], F32)
-            for i in range(passes):
-                matmul(bank[:], pre_out_q[0, 0], 0, pre_out_q[0, 0], 0, PASS, True, True)
-
         a_t = {}
 
+        a_banks = {}
+
+        def open_a(g, h):
+            a_banks[g, h] = [rotating("psum", "acc", 4, [P, PASS], F32) for t in range(4)]
+            for t in range(4):
+                matmul(a_banks[g, h][t][:], pre_out_q[0, h], P * t, mom_q[g, 0], 0, PASS, True, False)
+
+        def finish_a(g, h, t, bank):
+            matmul(bank[:], pre_out_q[1, h], P * t, mom_q[g, 1], 0, PASS, False, True)
+            if t == 0:
+                a_t[g, h] = rotating("sbuf", "a_t", 4, [P, 4, PASS], BF16)
+            nc.vector.scalar_tensor_tensor(
+                out=a_t[g, h][:, t, :],
+                in0=mom_t[g, h][:].rearrange("p (c t) -> p t c", t=4)[:, t, :],
+                scalar=damp_sb[:, h, t : t + 1],
+                in1=bank[:],
+                op0=MULT,
+                op1=ADD,
+            )
+
+        def close_a(g, h):
+            for t in range(4):
+                finish_a(g, h, t, a_banks[g, h][t])
+
         def product_a(g, h):
-            a_t[g, h] = rotating("sbuf", "a_t", 4, [P, 4, PASS], BF16)
-            mom_cols = mom_t[g, h][:].rearrange("p (c t) -> p t c", t=4)
             for t in range(4):
                 bank = rotating("psum", "acc", 4, [P, PASS], F32)
-                for kk in range(F_GROUPS):
-                    matmul(bank[:], pre_out_q[kk, h], P * t, mom_q[g, kk], 0, PASS, kk == 0, kk == F_GROUPS - 1)
-                nc.vector.scalar_tensor_tensor(
-                    out=a_t[g, h][:, t, :],
-                    in0=mom_cols[:, t, :],
-                    scalar=damp_sb[:, h, t : t + 1],
-                    in1=bank[:],
-                    op0=MULT,
-                    op1=ADD,
-                )
+                matmul(bank[:], pre_out_q[0, h], P * t, mom_q[g, 0], 0, PASS, True, False)
+                finish_a(g, h, t, bank)
 
         def turn_a(g, h):
             key = ("a", g, h)
@@ -196,63 +215,83 @@ def tile_preconditioned_momentum_outputs_h3_kernel(
 
         z_b = {}
 
-        def product_z(g, st):
-            bank = rotating("psum", "acc", 4, [P, 4, P], F32)
-            for t in range(4):
+        def product_z(g, slots):
+            for t in slots:
+                if t == 0:
+                    z_b[g] = rotating("sbuf", "z_b", 2, [P, 4, T], BF16)
+                bank = rotating("psum", "acc", 4, [P, T], F32)
                 for kk in range(D_GROUPS):
-                    matmul(bank[:, t, :], pre_in_q[g, kk], P * t, xt_q[kk], P * st, P, kk == 0, kk == D_GROUPS - 1)
-            z_b[g, st] = rotating("sbuf", "z_b", 3, [P, P * 4], BF16)
-            nc.vector.tensor_tensor(
-                out=z_b[g, st][:].rearrange("p (s t) -> p s t", t=4),
-                in0=bank[:].rearrange("p t s -> p s t"),
-                in1=lr_sb[:, g, :].unsqueeze(1).to_broadcast([P, P, 4]),
-                op=MULT,
-            )
+                    matmul(bank[:], pre_in_q[g, kk], P * t, xt_q[kk], 0, T, kk == 0, kk == D_GROUPS - 1)
+                nc.scalar.activation(out=z_b[g][:, t, :], in_=bank[:], func=COPY, scale=lr_f[:, g, t : t + 1])
 
-        def quantize_z(g, st):
-            quantize(z_q[g], z_b[g, st][:], P * st, P)
+        def weave_z(g, half):
+            dst = stage(("z", g))[:].rearrange("p (c i j) -> p c j i", i=4, j=4)
+            src = z_b[g][:].rearrange("p j (c i) -> p c j i", i=4)
+            nc.vector.tensor_copy(out=dst[:, 64 * half : 64 * (half + 1)], in_=src[:, 64 * half : 64 * (half + 1)])
+
+        def quantize_z(g, half):
+            quantize(z_q[g], grouped["z", g][:, 1024 * half : 1024 * (half + 1)], 256 * half, 256)
 
         y_b = {}
 
-        def product_y(st, h):
-            bank = rotating("psum", "acc", 4, [P, PASS], F32)
-            for g in range(D_GROUPS):
-                matmul(bank[:], z_q[g], P * st, a_q[g, h], 0, PASS, g == 0, g == D_GROUPS - 1)
-            y = rotating("sbuf", "y", 6, [P, PASS], F32)
+        y_banks, y_f = {}, {}
+
+        def open_y(st, h):
+            y_banks[st, h] = rotating("psum", "acc", 4, [P, PASS], F32)
+            for g in range(D_GROUPS - 1):
+                matmul(y_banks[st, h][:], z_q[g], P * st, a_q[g, h], 0, PASS, g == 0, False)
+
+        def close_y(st, h, last=False):
+            bank = y_banks[st, h]
+            matmul(bank[:], z_q[D_GROUPS - 1], P * st, a_q[D_GROUPS - 1, h], 0, PASS, False, True)
+            y = rotating("sbuf", "raw", LOAD_SLOTS, [P, PASS], F32)
+            y_b[st, h] = rotating("sbuf", "y_b", 8, [P, PASS], BF16)
+            sorted_b = y_b[st, h][:].rearrange("p (u m e) -> p u m e", u=2, e=2)
             cols = slice(PASS * h, PASS * (h + 1))
+            base_sb = raw["base", st // 2][:, st % 2, cols]
+            if last:
+                nc.vector.tensor_tensor(
+                    out=sorted_b,
+                    in0=base_sb.rearrange("p (m u e) -> p u m e", u=2, e=2),
+                    in1=bank[:].rearrange("p (u e m) -> p u m e", u=2, e=2),
+                    op=SUBTRACT,
+                )
             nc.vector.tensor_tensor(
                 out=y[:].rearrange("p (m t) -> p m t", t=4),
-                in0=raw["base", st // 2][:, st % 2, cols].rearrange("p (m t) -> p m t", t=4),
+                in0=base_sb.rearrange("p (m t) -> p m t", t=4),
                 in1=bank[:].rearrange("p (t m) -> p m t", t=4),
                 op=SUBTRACT,
             )
-            y_b[st, h] = rotating("sbuf", "y_b", 4, [P, PASS], BF16)
+            nc.sync.dma_start(out=out_0[P * st : P * (st + 1), cols], in_=y[:])
+            y_f[st, h] = y
+
+        def round_y(st, h):
             nc.scalar.copy(
                 out=y_b[st, h][:].rearrange("p (u m e) -> p u m e", u=2, e=2),
-                in_=y[:].rearrange("p (m u e) -> p u m e", u=2, e=2),
+                in_=y_f[st, h][:].rearrange("p (m u e) -> p u m e", u=2, e=2),
             )
-            nc.sync.dma_start(out=out_0[P * st : P * (st + 1), cols], in_=y[:])
 
         y_g = {}
 
-        def turn_y(st, h):
-            words = y_b[st, h][:].bitcast(F32)
-            bank = rotating("psum", "turn", 4, [P, 2, P], F32)
-            for u in range(2):
-                nc.tensor.transpose(bank[:, u, :], words[:, P * u : P * (u + 1)], ident[:])
-            y_g[st, h] = rotating("sbuf", "y_g", 4, [P, P * 4], BF16)
+        def turn_y(h, tiles):
+            n = len(tiles)
+            bank = rotating("psum", "turn", 4, [P, n, 2, P], F32)
+            for i, st in enumerate(tiles):
+                words = y_b[st, h][:].bitcast(F32)
+                for u in range(2):
+                    nc.tensor.transpose(bank[:, i, u, :], words[:, P * u : P * (u + 1)], ident[:])
+            y_g[h, tiles[0]] = rotating("sbuf", "y_g", 3, [P, n * P * 4], BF16)
             nc.scalar.copy(
-                out=y_g[st, h][:].bitcast(F32).rearrange("p (s u) -> p s u", u=2),
-                in_=bank[:].rearrange("p u s -> p s u"),
+                out=y_g[h, tiles[0]][:].bitcast(F32).rearrange("p (i s u) -> p i s u", i=n, u=2),
+                in_=bank[:].rearrange("p i u s -> p i s u"),
             )
 
-        def quantize_y(st, h):
-            quantize((y_codes[st][:, h, :], y_scales[:, h, P * st : P * (st + 1)]), y_g[st, h][:], 0, P)
-
-        def store_words(st):
-            cols = slice(P * st, P * (st + 1))
-            words = out_1.rearrange("h p s b -> p h (s b)").bitcast(I32)
-            nc.sync.dma_start(out=words[:, :, cols], in_=y_codes[st][:].bitcast(I32))
+        def planes_y(h, tiles):
+            cols = slice(P * tiles[0], P * (tiles[-1] + 1))
+            codes = rotating("sbuf", "y_codes", 5, [P, len(tiles) * P], U32)
+            quantize((codes, y_scales[:, h, cols]), y_g[h, tiles[0]][:], 0, len(tiles) * P)
+            words = out_1[h].rearrange("p s b -> p (s b)").bitcast(I32)
+            nc.sync.dma_start(out=words[:, cols], in_=codes[:].bitcast(I32))
 
         def store_scales():
             for q in range(4):
@@ -268,12 +307,12 @@ def tile_preconditioned_momentum_outputs_h3_kernel(
         load_pre_out(0, 0)
         load_mom(0, 1)
         load_pre_out(1, 0)
+        with nc.allow_non_contiguous_dma(reason="one short run of a vector to each partition"):
+            nc.sync.dma_start(out=damp_sb[:], in_=damp.rearrange("(h p t) -> p h t", p=P, t=4))
         load_mom(1, 0)
         load_mom(1, 1)
         load_pre_out(0, 1)
         load_mom(2, 0)
-        with nc.allow_non_contiguous_dma(reason="one short run of a vector to each partition"):
-            nc.sync.dma_start(out=damp_sb[:], in_=damp.rearrange("(h p t) -> p h t", p=P, t=4))
         load_mom(2, 1)
         load_pre_in(0, 0)
         load_pre_out(1, 1)
@@ -283,100 +322,108 @@ def tile_preconditioned_momentum_outputs_h3_kernel(
             load_xt(kk)
 
         turn_mom(0, 0)
-        weave_pre_out("vector", 0, 0, 0)
-        weave_pre_out("vector", 0, 0, 1)
-        turn_mom(0, 1)
-        quantize(pre_out_q[0, 0], grouped["pre_out", 0, 0][:])
-        weave_pre_out("vector", 1, 0, 0)
-        weave_pre_out("scalar", 1, 0, 1)
+        weave_pre_out("vector", 0, 0, 0, 4)
         quantize(mom_q[0, 0], mom_t[0, 0][:])
+        quantize(pre_out_q[0, 0], grouped["pre_out", 0, 0][:])
+        turn_mom(0, 1)
+        open_a(0, 0)
+        weave_pre_out("vector", 1, 0, 0, 4)
         quantize(mom_q[0, 1], mom_t[0, 1][:])
         quantize(pre_out_q[1, 0], grouped["pre_out", 1, 0][:])
-        warm_up(2)
         turn_mom(1, 0)
         with nc.allow_non_contiguous_dma(reason="one short run of a vector to each partition"):
             nc.sync.dma_start(out=lr_sb[:], in_=lr.rearrange("(g p t) -> p g t", p=P, t=4))
         for kk in range(3):
             load_pre_in(1, kk)
-        warm_up(2)
-        turn_mom(1, 1)
+        close_a(0, 0)
         quantize(mom_q[1, 0], mom_t[1, 0][:])
+        turn_mom(1, 1)
         quantize(mom_q[1, 1], mom_t[1, 1][:])
-        weave_pre_out("scalar", 0, 1, 0)
-        weave_pre_out("scalar", 0, 1, 1)
-        product_a(0, 0)
         turn_mom(2, 0)
+        weave_pre_out("scalar", 0, 1, 0, 2)
+        weave_pre_out("scalar", 0, 1, 2, 4)
+        quantize(mom_q[2, 0], mom_t[2, 0][:])
+        product_a(1, 0)
         turn_mom(2, 1)
         for kk in range(3):
             load_pre_in(2, kk)
         quantize(pre_out_q[0, 1], grouped["pre_out", 0, 1][:])
-        weave_pre_out("scalar", 1, 1, 0)
-        weave_pre_out("scalar", 1, 1, 1)
-        quantize(mom_q[2, 0], mom_t[2, 0][:])
         quantize(mom_q[2, 1], mom_t[2, 1][:])
-        product_a(1, 0)
         turn_pre_in(0, 0)
+        weave_pre_out("scalar", 1, 1, 0, 2)
+        weave_pre_out("scalar", 1, 1, 2, 4)
         load_base(0)
         load_base(1)
-        weave_xt("scalar", 0, 0)
-        weave_xt("scalar", 0, 1)
-        quantize(pre_out_q[1, 1], grouped["pre_out", 1, 1][:])
         product_a(2, 0)
+        quantize(pre_out_q[1, 1], grouped["pre_out", 1, 1][:])
         turn_pre_in(0, 1)
         turn_pre_in(0, 2)
+        weave_xt("scalar", 0, 0)
+        weave_xt("scalar", 0, 1)
+        product_a(0, 1)
         quantize(xt_q[0], grouped["xt", 0][:])
+        turn_a(0, 0)
+        weave_xt("vector", 2, 0)
+        turn_pre_in(1, 0)
         weave_xt("scalar", 1, 0)
         weave_xt("scalar", 1, 1)
-        product_a(0, 1)
-        turn_a(0, 0)
-        turn_pre_in(1, 0)
-        quantize(xt_q[1], grouped["xt", 1][:])
-        weave_xt("scalar", 2, 0)
-        weave_xt("scalar", 2, 1)
         product_a(1, 1)
+        quantize(xt_q[1], grouped["xt", 1][:])
         turn_a(1, 0)
+        weave_xt("vector", 2, 1)
+        nc.vector.tensor_copy(out=lr_f[:], in_=lr_sb[:])
         turn_pre_in(1, 1)
         quantize(xt_q[2], grouped["xt", 2][:])
         product_a(2, 1)
         turn_a(2, 0)
         turn_pre_in(1, 2)
-        for st in range(4):
-            product_z(0, st)
-            if st > 0:
-                quantize_z(0, st - 1)
-        turn_pre_in(2, 0)
-        quantize_z(0, 3)
+        for kk in range(3):
+            sort_pre_in("vector", 2, kk)
+        product_z(0, range(4))
         turn_a(0, 1)
-        product_z(1, 0)
-        product_z(1, 1)
-        quantize_z(1, 0)
+        turn_pre_in(2, 0)
+        weave_z(0, 0)
+        weave_z(0, 1)
+        product_z(1, range(2))
+        quantize_z(0, 0)
+        quantize_z(0, 1)
         turn_pre_in(2, 1)
-        quantize_z(1, 1)
         turn_pre_in(2, 2)
-        product_z(1, 2)
-        product_z(1, 3)
-        quantize_z(1, 2)
+        product_z(1, range(2, 4))
         turn_a(1, 1)
-        quantize_z(1, 3)
-        turn_a(2, 1)
-        product_z(2, 0)
-        product_z(2, 1)
+        weave_z(1, 0)
+        weave_z(1, 1)
+        product_z(2, range(4))
+        quantize_z(1, 0)
+        quantize_z(1, 1)
+        weave_z(2, 0)
+        weave_z(2, 1)
         quantize_z(2, 0)
-        product_z(2, 2)
         quantize_z(2, 1)
-        product_y(0, 0)
-        quantize_z(2, 2)
-        product_z(2, 3)
-        product_y(0, 1)
-        quantize_z(2, 3)
-        product_y(1, 0)
-        product_y(1, 1)
-        for st in range(2, 6):
-            for h in range(2):
-                turn_y(st - 2, h)
-            for h in range(2):
-                if st < 4:
-                    product_y(st, h)
-                quantize_y(st - 2, h)
-            store_words(st - 2)
+        turn_a(2, 1)
+        for st in range(4):
+            open_y(st, 0)
+        for st in range(4):
+            close_y(st, 0)
+            round_y(st, 0)
+        for st in range(2):
+            open_y(st, 1)
+            close_y(st, 1)
+        turn_y(0, [0, 1])
+        turn_y(0, [2, 3])
+        round_y(0, 1)
+        round_y(1, 1)
+        planes_y(0, [0, 1])
+        planes_y(0, [2, 3])
+        open_y(2, 1)
+        close_y(2, 1)
+        round_y(2, 1)
+        open_y(3, 1)
+        close_y(3, 1, last=True)
+        turn_y(1, [0, 1])
+        turn_y(1, [2])
+        turn_y(1, [3])
+        planes_y(1, [0, 1])
+        planes_y(1, [2])
+        planes_y(1, [3])
         store_scales()

@@ -106,7 +106,7 @@ def tile_preconditioned_momentum_outputs_h3_kernel(
             for h in range(F_GROUPS):
                 mom_q[g, h] = operand("mom%d%d" % (g, h))
                 a_q[g, h] = operand("a%d%d" % (g, h))
-                mom_t[g, h] = keep.tile([P, PASS * 4], BF16, name="mom_t%d%d" % (g, h), align_bytes=ALIGN)
+                mom_t[g, h] = keep.tile([P, PASS * 4], BF16, name="mom_t%d%d" % (g, h), tag="mom_t%d%d" % (g, h), align_bytes=ALIGN)
         for kk in range(F_GROUPS):
             for h in range(F_GROUPS):
                 pre_out_q[kk, h] = operand("pre_out%d%d" % (kk, h))
@@ -119,10 +119,20 @@ def tile_preconditioned_momentum_outputs_h3_kernel(
             else:
                 nc.scalar.copy(out=out, in_=in_)
 
+        free_slots = list(range(6))
+        slot_of = {}
+
         def stage(key):
             if key not in grouped:
-                grouped[key] = rotating("sbuf", "grouped", 6, [P, PASS * 4], BF16)
+                slot_of[key] = free_slots[0]
+                free_slots.remove(slot_of[key])
+                name = "grouped%d" % slot_of[key]
+                grouped[key] = keep.tile([P, PASS * 4], BF16, name=name, tag=name, align_bytes=ALIGN)
             return grouped[key]
+
+        def quantize_staged(q, key):
+            quantize(q, grouped[key][:])
+            free_slots.append(slot_of[key])
 
         def weave_pre_out(engine, kk, h, t0, t1):
             key = ("pre_out", kk, h)
@@ -130,11 +140,11 @@ def tile_preconditioned_momentum_outputs_h3_kernel(
             src = raw[key][:].rearrange("p j (m t) -> p t m j", t=4)
             copy_on(engine, dst[:, t0:t1], src[:, t0:t1])
 
-        def weave_xt(engine, kk, half):
+        def weave_xt(engine, kk, q0, q1):
             key = ("xt", kk)
             dst = stage(key)[:].rearrange("p (c i j) -> p c j i", i=4, j=4)
             src = raw[key][:].rearrange("p j (c i) -> p c j i", i=4)
-            copy_on(engine, dst[:, 64 * half : 64 * (half + 1)], src[:, 64 * half : 64 * (half + 1)])
+            copy_on(engine, dst[:, 32 * q0 : 32 * q1], src[:, 32 * q0 : 32 * q1])
 
         def turn_mom(g, kk):
             words = raw["mom", g, kk][:].bitcast(F32)
@@ -146,20 +156,9 @@ def tile_preconditioned_momentum_outputs_h3_kernel(
                         nc.tensor.transpose(bank[:, e, w, :], words[:, 2 * u + e, w:256:2], ident[:])
                 nc.scalar.copy(out=dst[:, u], in_=bank[:].rearrange("p e w m -> p m e w"))
 
-        halves = {}
-
-        def sort_pre_in(engine, g, kk):
-            key = ("pre_in", g, kk)
-            halves[key] = rotating("sbuf", "raw", LOAD_SLOTS, [P, 4, 2, P], F32)
-            src = raw[key][:].bitcast(F32).rearrange("p t (c i w) -> p t c w i", i=4, w=2)
-            copy_on(engine, halves[key][:].rearrange("p t w (c i) -> p t c w i", i=4), src)
-
         def turn_pre_in(g, kk):
             key = ("pre_in", g, kk)
-            if key in halves:
-                words = halves[key]
-            else:
-                words = raw[key][:].bitcast(F32).rearrange("p t (m w) -> p t w m", w=2)
+            words = raw[key][:].bitcast(F32).rearrange("p t (m w) -> p t w m", w=2)
             dst = stage(key)[:].bitcast(F32).rearrange("p (t m w) -> p t m w", t=4, w=2)
             for v in range(2):
                 bank = rotating("psum", "turn", 4, [P, 2, 2, P], F32)
@@ -167,7 +166,6 @@ def tile_preconditioned_momentum_outputs_h3_kernel(
                     for w in range(2):
                         nc.tensor.transpose(bank[:, e, w, :], words[:, 2 * v + e, w, :], ident[:])
                 nc.scalar.copy(out=dst[:, 2 * v : 2 * v + 2], in_=bank[:].rearrange("p e w m -> p e m w"))
-            quantize(pre_in_q[g, kk], grouped[key][:])
 
         a_t = {}
 
@@ -181,7 +179,7 @@ def tile_preconditioned_momentum_outputs_h3_kernel(
         def finish_a(g, h, t, bank):
             matmul(bank[:], pre_out_q[1, h], P * t, mom_q[g, 1], 0, PASS, False, True)
             if t == 0:
-                a_t[g, h] = rotating("sbuf", "a_t", 4, [P, 4, PASS], BF16)
+                a_t[g, h] = rotating("sbuf", "a_t", 6, [P, 4, PASS], BF16)
             nc.vector.scalar_tensor_tensor(
                 out=a_t[g, h][:, t, :],
                 in0=mom_t[g, h][:].rearrange("p (c t) -> p t c", t=4)[:, t, :],
@@ -195,13 +193,13 @@ def tile_preconditioned_momentum_outputs_h3_kernel(
             for t in range(4):
                 finish_a(g, h, t, a_banks[g, h][t])
 
-        def product_a(g, h):
-            for t in range(4):
+        def product_a(g, h, slots=range(4)):
+            for t in slots:
                 bank = rotating("psum", "acc", 4, [P, PASS], F32)
                 matmul(bank[:], pre_out_q[0, h], P * t, mom_q[g, 0], 0, PASS, True, False)
                 finish_a(g, h, t, bank)
 
-        def turn_a(g, h):
+        def turn_a(g, h, last_bank):
             key = ("a", g, h)
             words = a_t[g, h][:].bitcast(F32)
             dst = stage(key)[:].bitcast(F32).rearrange("p (t m u) -> p t m u", t=4, u=2)
@@ -210,27 +208,28 @@ def tile_preconditioned_momentum_outputs_h3_kernel(
                 for e in range(2):
                     for u in range(2):
                         nc.tensor.transpose(bank[:, e, u, :], words[:, 2 * v + e, P * u : P * (u + 1)], ident[:])
-                nc.scalar.copy(out=dst[:, 2 * v : 2 * v + 2], in_=bank[:].rearrange("p e u m -> p e m u"))
-            quantize(a_q[g, h], grouped[key][:])
+                copy_on(("scalar", last_bank)[v], dst[:, 2 * v : 2 * v + 2], bank[:].rearrange("p e u m -> p e m u"))
 
         z_b = {}
 
         def product_z(g, slots):
             for t in slots:
                 if t == 0:
-                    z_b[g] = rotating("sbuf", "z_b", 2, [P, 4, T], BF16)
+                    z_b[g] = keep.tile([P, 4, T], BF16, name="z_b%d" % g, tag="mom_t%d0" % g, align_bytes=ALIGN)
                 bank = rotating("psum", "acc", 4, [P, T], F32)
                 for kk in range(D_GROUPS):
                     matmul(bank[:], pre_in_q[g, kk], P * t, xt_q[kk], 0, T, kk == 0, kk == D_GROUPS - 1)
                 nc.scalar.activation(out=z_b[g][:, t, :], in_=bank[:], func=COPY, scale=lr_f[:, g, t : t + 1])
 
-        def weave_z(g, half):
+        def weave_z(engine, g, half):
             dst = stage(("z", g))[:].rearrange("p (c i j) -> p c j i", i=4, j=4)
             src = z_b[g][:].rearrange("p j (c i) -> p c j i", i=4)
-            nc.vector.tensor_copy(out=dst[:, 64 * half : 64 * (half + 1)], in_=src[:, 64 * half : 64 * (half + 1)])
+            copy_on(engine, dst[:, 64 * half : 64 * (half + 1)], src[:, 64 * half : 64 * (half + 1)])
 
         def quantize_z(g, half):
             quantize(z_q[g], grouped["z", g][:, 1024 * half : 1024 * (half + 1)], 256 * half, 256)
+            if half == 1:
+                free_slots.append(slot_of["z", g])
 
         y_b = {}
 
@@ -309,98 +308,84 @@ def tile_preconditioned_momentum_outputs_h3_kernel(
         load_pre_out(1, 0)
         with nc.allow_non_contiguous_dma(reason="one short run of a vector to each partition"):
             nc.sync.dma_start(out=damp_sb[:], in_=damp.rearrange("(h p t) -> p h t", p=P, t=4))
+            nc.sync.dma_start(out=lr_sb[:], in_=lr.rearrange("(g p t) -> p g t", p=P, t=4))
         load_mom(1, 0)
         load_mom(1, 1)
-        load_pre_out(0, 1)
         load_mom(2, 0)
+        load_pre_out(0, 1)
         load_mom(2, 1)
         load_pre_in(0, 0)
         load_pre_out(1, 1)
         load_pre_in(0, 1)
         load_pre_in(0, 2)
-        for kk in range(3):
-            load_xt(kk)
+        load_xt(0)
+        load_pre_in(1, 0)
+        load_pre_in(1, 1)
 
         turn_mom(0, 0)
-        weave_pre_out("vector", 0, 0, 0, 4)
+        weave_pre_out("vector", 0, 0, 0, 2)
+        weave_pre_out("scalar", 0, 0, 2, 4)
         quantize(mom_q[0, 0], mom_t[0, 0][:])
-        quantize(pre_out_q[0, 0], grouped["pre_out", 0, 0][:])
+        quantize_staged(pre_out_q[0, 0], ("pre_out", 0, 0))
         turn_mom(0, 1)
         open_a(0, 0)
-        weave_pre_out("vector", 1, 0, 0, 4)
+        weave_pre_out("vector", 1, 0, 0, 2)
+        weave_pre_out("scalar", 1, 0, 2, 4)
         quantize(mom_q[0, 1], mom_t[0, 1][:])
-        quantize(pre_out_q[1, 0], grouped["pre_out", 1, 0][:])
+        quantize_staged(pre_out_q[1, 0], ("pre_out", 1, 0))
         turn_mom(1, 0)
-        with nc.allow_non_contiguous_dma(reason="one short run of a vector to each partition"):
-            nc.sync.dma_start(out=lr_sb[:], in_=lr.rearrange("(g p t) -> p g t", p=P, t=4))
-        for kk in range(3):
-            load_pre_in(1, kk)
+        load_xt(1)
+        load_pre_in(1, 2)
+        load_pre_in(2, 0)
+        load_xt(2)
+        load_pre_in(2, 1)
         close_a(0, 0)
         quantize(mom_q[1, 0], mom_t[1, 0][:])
         turn_mom(1, 1)
-        quantize(mom_q[1, 1], mom_t[1, 1][:])
         turn_mom(2, 0)
-        weave_pre_out("scalar", 0, 1, 0, 2)
-        weave_pre_out("scalar", 0, 1, 2, 4)
+        load_pre_in(2, 2)
+        load_base(0)
+        quantize(mom_q[1, 1], mom_t[1, 1][:])
         quantize(mom_q[2, 0], mom_t[2, 0][:])
+        nc.scalar.copy(out=lr_f[:], in_=lr_sb[:])
+        weave_pre_out("scalar", 0, 1, 0, 4)
+        load_base(1)
         product_a(1, 0)
         turn_mom(2, 1)
-        for kk in range(3):
-            load_pre_in(2, kk)
-        quantize(pre_out_q[0, 1], grouped["pre_out", 0, 1][:])
-        quantize(mom_q[2, 1], mom_t[2, 1][:])
         turn_pre_in(0, 0)
-        weave_pre_out("scalar", 1, 1, 0, 2)
-        weave_pre_out("scalar", 1, 1, 2, 4)
-        load_base(0)
-        load_base(1)
+        quantize_staged(pre_out_q[0, 1], ("pre_out", 0, 1))
+        quantize(mom_q[2, 1], mom_t[2, 1][:])
+        quantize_staged(pre_in_q[0, 0], ("pre_in", 0, 0))
+        weave_pre_out("scalar", 1, 1, 0, 4)
         product_a(2, 0)
-        quantize(pre_out_q[1, 1], grouped["pre_out", 1, 1][:])
-        turn_pre_in(0, 1)
-        turn_pre_in(0, 2)
-        weave_xt("scalar", 0, 0)
-        weave_xt("scalar", 0, 1)
-        product_a(0, 1)
-        quantize(xt_q[0], grouped["xt", 0][:])
-        turn_a(0, 0)
-        weave_xt("vector", 2, 0)
-        turn_pre_in(1, 0)
-        weave_xt("scalar", 1, 0)
-        weave_xt("scalar", 1, 1)
-        product_a(1, 1)
-        quantize(xt_q[1], grouped["xt", 1][:])
-        turn_a(1, 0)
-        weave_xt("vector", 2, 1)
-        nc.vector.tensor_copy(out=lr_f[:], in_=lr_sb[:])
-        turn_pre_in(1, 1)
-        quantize(xt_q[2], grouped["xt", 2][:])
-        product_a(2, 1)
-        turn_a(2, 0)
-        turn_pre_in(1, 2)
-        for kk in range(3):
-            sort_pre_in("vector", 2, kk)
-        product_z(0, range(4))
-        turn_a(0, 1)
-        turn_pre_in(2, 0)
-        weave_z(0, 0)
-        weave_z(0, 1)
-        product_z(1, range(2))
-        quantize_z(0, 0)
-        quantize_z(0, 1)
+        quantize_staged(pre_out_q[1, 1], ("pre_out", 1, 1))
+        for g in range(3):
+            first, second = divmod(2 * g + 1, 3), divmod(2 * g + 2, 3)
+            turn_pre_in(*first)
+            turn_pre_in(*second)
+            quantize_staged(pre_in_q[first], ("pre_in", *first))
+            weave_xt("vector", g, 3, 4)
+            quantize_staged(pre_in_q[second], ("pre_in", *second))
+            weave_xt("scalar", g, 0, 3)
+            product_a(g, 1, range(2))
+            quantize_staged(xt_q[g], ("xt", g))
+            product_a(g, 1, range(2, 4))
         turn_pre_in(2, 1)
         turn_pre_in(2, 2)
-        product_z(1, range(2, 4))
-        turn_a(1, 1)
-        weave_z(1, 0)
-        weave_z(1, 1)
-        product_z(2, range(4))
-        quantize_z(1, 0)
-        quantize_z(1, 1)
-        weave_z(2, 0)
-        weave_z(2, 1)
-        quantize_z(2, 0)
-        quantize_z(2, 1)
-        turn_a(2, 1)
+        quantize_staged(pre_in_q[2, 1], ("pre_in", 2, 1))
+        quantize_staged(pre_in_q[2, 2], ("pre_in", 2, 2))
+        a_order = [(g, h) for h in range(2) for g in range(3)]
+        for g in range(3):
+            product_z(g, range(4))
+            first, second = a_order[2 * g], a_order[2 * g + 1]
+            turn_a(*first, "scalar")
+            weave_z("vector", g, 0)
+            turn_a(*second, "vector" if g < 2 else "scalar")
+            weave_z("vector", g, 1)
+            quantize_z(g, 0)
+            quantize_z(g, 1)
+            quantize_staged(a_q[first], ("a", *first))
+            quantize_staged(a_q[second], ("a", *second))
         for st in range(4):
             open_y(st, 0)
         for st in range(4):

@@ -22,7 +22,7 @@ PASS = 512
 D_GROUPS = D // PASS
 F_GROUPS = F // PASS
 S_TILES = T // P
-LOAD_SLOTS = 16
+LOAD_SLOTS = 12
 ALIGN = 64
 
 
@@ -70,27 +70,28 @@ def tile_preconditioned_momentum_outputs_h3_kernel(
 
         raw = {}
 
-        def load(key, src):
-            raw[key] = rotating("sbuf", "raw", LOAD_SLOTS, list(src.shape), BF16)
+        def load(key, src, slot):
+            raw[key] = keep.tile(list(src.shape), BF16, name="raw_" + slot, tag=slot, align_bytes=ALIGN)
             nc.sync.dma_start(out=raw[key][:], in_=src)
 
-        def load_mom(g, kk):
-            rows = mom[PASS * g : PASS * (g + 1), PASS * kk : PASS * (kk + 1)]
-            load(("mom", g, kk), rows.rearrange("(m t) k -> m t k", t=4))
+        def load_mom(g, u):
+            rows = mom[PASS * g : PASS * (g + 1), :].rearrange("(m t) k -> m t k", t=4)
+            load(("mom", g, u), rows[:, 2 * u : 2 * u + 2, :], "slot%d" % (2 * g + u))
 
-        def load_pre_out(kk, h):
-            rows = pre_out[PASS * kk : PASS * (kk + 1), PASS * h : PASS * (h + 1)]
-            load(("pre_out", kk, h), rows.rearrange("(p j) c -> p j c", j=4))
+        def load_pre_out(kk):
+            rows = pre_out[PASS * kk : PASS * (kk + 1), :]
+            load(("pre_out", kk), rows.rearrange("(p j) c -> p j c", j=4), "wide%d" % kk)
 
-        def load_pre_in(g, kk):
-            rows = pre_in[PASS * g : PASS * (g + 1), PASS * kk : PASS * (kk + 1)]
-            load(("pre_in", g, kk), rows.rearrange("(m t) k -> m t k", t=4))
+        def load_pre_in(g, v):
+            rows = pre_in[PASS * g : PASS * (g + 1), :].rearrange("(m t) k -> m t k", t=4)
+            slot = "wide%d" % v if g == D_GROUPS - 1 else "mid%d" % (2 * g + v)
+            load(("pre_in", g, v), rows[:, 2 * v : 2 * v + 2, :], slot)
 
         def load_xt(kk):
-            load(("xt", kk), xt[PASS * kk : PASS * (kk + 1), :].rearrange("(p j) s -> p j s", j=4))
+            load(("xt", kk), xt[PASS * kk : PASS * (kk + 1), :].rearrange("(p j) s -> p j s", j=4), "slot%d" % kk)
 
         def load_base(i):
-            load(("base", i), base[2 * P * i : 2 * P * (i + 1), :].rearrange("(a p) f -> p a f", p=P))
+            load(("base", i), base[2 * P * i : 2 * P * (i + 1), :].rearrange("(a p) f -> p a f", p=P), "slot%d" % (3 + i))
 
         ident = keep.tile([P, P], F32, name="ident")
         damp_sb = keep.tile([P, F_GROUPS, 4], BF16, name="damp_sb")
@@ -137,7 +138,7 @@ def tile_preconditioned_momentum_outputs_h3_kernel(
         def weave_pre_out(engine, kk, h, t0, t1):
             key = ("pre_out", kk, h)
             dst = stage(key)[:].rearrange("p (t m j) -> p t m j", t=4, j=4)
-            src = raw[key][:].rearrange("p j (m t) -> p t m j", t=4)
+            src = raw["pre_out", kk][:, :, PASS * h : PASS * (h + 1)].rearrange("p j (m t) -> p t m j", t=4)
             copy_on(engine, dst[:, t0:t1], src[:, t0:t1])
 
         def weave_xt(engine, kk, q0, q1):
@@ -146,25 +147,24 @@ def tile_preconditioned_momentum_outputs_h3_kernel(
             src = raw[key][:].rearrange("p j (c i) -> p c j i", i=4)
             copy_on(engine, dst[:, 32 * q0 : 32 * q1], src[:, 32 * q0 : 32 * q1])
 
-        def turn_mom(g, kk):
-            words = raw["mom", g, kk][:].bitcast(F32)
-            dst = mom_t[g, kk][:].bitcast(F32).rearrange("p (u m e w) -> p u m e w", u=2, e=2, w=2)
-            for u in range(2):
+        def turn_mom(g, u):
+            words = raw["mom", g, u][:].bitcast(F32)
+            for kk in range(F_GROUPS):
                 bank = rotating("psum", "turn", 4, [P, 2, 2, P], F32)
                 for e in range(2):
                     for w in range(2):
-                        nc.tensor.transpose(bank[:, e, w, :], words[:, 2 * u + e, w:256:2], ident[:])
+                        nc.tensor.transpose(bank[:, e, w, :], words[:, e, 256 * kk + w : 256 * (kk + 1) : 2], ident[:])
+                dst = mom_t[g, kk][:].bitcast(F32).rearrange("p (u m e w) -> p u m e w", u=2, e=2, w=2)
                 nc.scalar.copy(out=dst[:, u], in_=bank[:].rearrange("p e w m -> p m e w"))
 
         def turn_pre_in(g, kk):
-            key = ("pre_in", g, kk)
-            words = raw[key][:].bitcast(F32).rearrange("p t (m w) -> p t w m", w=2)
-            dst = stage(key)[:].bitcast(F32).rearrange("p (t m w) -> p t m w", t=4, w=2)
+            dst = stage(("pre_in", g, kk))[:].bitcast(F32).rearrange("p (t m w) -> p t m w", t=4, w=2)
             for v in range(2):
+                words = raw["pre_in", g, v][:].bitcast(F32)
                 bank = rotating("psum", "turn", 4, [P, 2, 2, P], F32)
                 for e in range(2):
                     for w in range(2):
-                        nc.tensor.transpose(bank[:, e, w, :], words[:, 2 * v + e, w, :], ident[:])
+                        nc.tensor.transpose(bank[:, e, w, :], words[:, e, 256 * kk + w : 256 * (kk + 1) : 2], ident[:])
                 nc.scalar.copy(out=dst[:, 2 * v : 2 * v + 2], in_=bank[:].rearrange("p e w m -> p e m w"))
 
         a_t = {}
@@ -189,8 +189,8 @@ def tile_preconditioned_momentum_outputs_h3_kernel(
                 op1=ADD,
             )
 
-        def close_a(g, h):
-            for t in range(4):
+        def close_a(g, h, slots):
+            for t in slots:
                 finish_a(g, h, t, a_banks[g, h][t])
 
         def product_a(g, h, slots=range(4)):
@@ -243,7 +243,7 @@ def tile_preconditioned_momentum_outputs_h3_kernel(
         def close_y(st, h, last=False):
             bank = y_banks[st, h]
             matmul(bank[:], z_q[D_GROUPS - 1], P * st, a_q[D_GROUPS - 1, h], 0, PASS, False, True)
-            y = rotating("sbuf", "raw", LOAD_SLOTS, [P, PASS], F32)
+            y = keep.tile([P, PASS], F32, name="y", tag=("mid%d", "slot%d")[h] % (st if st < 3 or h == 0 else 5), align_bytes=ALIGN)
             y_b[st, h] = rotating("sbuf", "y_b", 8, [P, PASS], BF16)
             sorted_b = y_b[st, h][:].rearrange("p (u m e) -> p u m e", u=2, e=2)
             cols = slice(PASS * h, PASS * (h + 1))
@@ -303,89 +303,111 @@ def tile_preconditioned_momentum_outputs_h3_kernel(
 
         make_identity(nc, ident[:])
         load_mom(0, 0)
-        load_pre_out(0, 0)
         load_mom(0, 1)
-        load_pre_out(1, 0)
+        load_pre_out(0)
+        load_mom(1, 0)
+        load_pre_out(1)
         with nc.allow_non_contiguous_dma(reason="one short run of a vector to each partition"):
             nc.sync.dma_start(out=damp_sb[:], in_=damp.rearrange("(h p t) -> p h t", p=P, t=4))
             nc.sync.dma_start(out=lr_sb[:], in_=lr.rearrange("(g p t) -> p g t", p=P, t=4))
-        load_mom(1, 0)
         load_mom(1, 1)
         load_mom(2, 0)
-        load_pre_out(0, 1)
         load_mom(2, 1)
-        load_pre_in(0, 0)
-        load_pre_out(1, 1)
-        load_pre_in(0, 1)
-        load_pre_in(0, 2)
-        load_xt(0)
-        load_pre_in(1, 0)
-        load_pre_in(1, 1)
 
         turn_mom(0, 0)
+        turn_mom(0, 1)
+        quantize(mom_q[0, 0], mom_t[0, 0][:])
+        quantize(mom_q[0, 1], mom_t[0, 1][:])
         weave_pre_out("vector", 0, 0, 0, 2)
         weave_pre_out("scalar", 0, 0, 2, 4)
-        quantize(mom_q[0, 0], mom_t[0, 0][:])
         quantize_staged(pre_out_q[0, 0], ("pre_out", 0, 0))
-        turn_mom(0, 1)
+        turn_mom(1, 0)
+        load_xt(0)
+        load_pre_in(0, 0)
+        load_pre_in(0, 1)
+        load_xt(1)
+        load_pre_in(1, 0)
+        load_pre_in(1, 1)
+        load_xt(2)
+        weave_pre_out("vector", 0, 1, 0, 4)
         open_a(0, 0)
         weave_pre_out("vector", 1, 0, 0, 2)
         weave_pre_out("scalar", 1, 0, 2, 4)
-        quantize(mom_q[0, 1], mom_t[0, 1][:])
-        quantize_staged(pre_out_q[1, 0], ("pre_out", 1, 0))
-        turn_mom(1, 0)
-        load_xt(1)
-        load_pre_in(1, 2)
-        load_pre_in(2, 0)
-        load_xt(2)
-        load_pre_in(2, 1)
-        close_a(0, 0)
-        quantize(mom_q[1, 0], mom_t[1, 0][:])
-        turn_mom(1, 1)
-        turn_mom(2, 0)
-        load_pre_in(2, 2)
-        load_base(0)
-        quantize(mom_q[1, 1], mom_t[1, 1][:])
-        quantize(mom_q[2, 0], mom_t[2, 0][:])
-        nc.scalar.copy(out=lr_f[:], in_=lr_sb[:])
-        weave_pre_out("scalar", 0, 1, 0, 4)
-        load_base(1)
-        product_a(1, 0)
-        turn_mom(2, 1)
-        turn_pre_in(0, 0)
         quantize_staged(pre_out_q[0, 1], ("pre_out", 0, 1))
-        quantize(mom_q[2, 1], mom_t[2, 1][:])
-        quantize_staged(pre_in_q[0, 0], ("pre_in", 0, 0))
-        weave_pre_out("scalar", 1, 1, 0, 4)
-        product_a(2, 0)
+        quantize_staged(pre_out_q[1, 0], ("pre_out", 1, 0))
+        weave_pre_out("scalar", 1, 1, 0, 2)
+        weave_pre_out("vector", 1, 1, 2, 4)
+        turn_mom(1, 1)
+        nc.scalar.copy(out=lr_f[:], in_=lr_sb[:])
         quantize_staged(pre_out_q[1, 1], ("pre_out", 1, 1))
-        for g in range(3):
-            first, second = divmod(2 * g + 1, 3), divmod(2 * g + 2, 3)
-            turn_pre_in(*first)
-            turn_pre_in(*second)
-            quantize_staged(pre_in_q[first], ("pre_in", *first))
-            weave_xt("vector", g, 3, 4)
-            quantize_staged(pre_in_q[second], ("pre_in", *second))
-            weave_xt("scalar", g, 0, 3)
-            product_a(g, 1, range(2))
-            quantize_staged(xt_q[g], ("xt", g))
-            product_a(g, 1, range(2, 4))
+        close_a(0, 0, range(4))
+        turn_mom(2, 0)
+        turn_mom(2, 1)
+        load_pre_in(2, 0)
+        load_pre_in(2, 1)
+        load_base(0)
+        load_base(1)
+        quantize(mom_q[1, 0], mom_t[1, 0][:])
+        quantize(mom_q[1, 1], mom_t[1, 1][:])
+        weave_xt("scalar", 0, 0, 4)
+        product_a(0, 1)
+        turn_pre_in(0, 0)
+        turn_pre_in(0, 1)
+        quantize_staged(xt_q[0], ("xt", 0))
+        quantize_staged(pre_in_q[0, 0], ("pre_in", 0, 0))
+        quantize_staged(pre_in_q[0, 1], ("pre_in", 0, 1))
+        weave_xt("scalar", 1, 0, 4)
+        product_a(1, 0)
+        turn_pre_in(0, 2)
+        turn_pre_in(1, 0)
+        quantize_staged(xt_q[1], ("xt", 1))
+        quantize_staged(pre_in_q[0, 2], ("pre_in", 0, 2))
+        quantize_staged(pre_in_q[1, 0], ("pre_in", 1, 0))
+        weave_xt("scalar", 2, 0, 4)
+        product_a(1, 1, range(2))
+        quantize_staged(xt_q[2], ("xt", 2))
+        product_a(1, 1, range(2, 4))
+        turn_pre_in(1, 1)
+        turn_pre_in(1, 2)
+        quantize(mom_q[2, 0], mom_t[2, 0][:])
+        quantize(mom_q[2, 1], mom_t[2, 1][:])
+        product_z(0, range(4))
+        quantize_staged(pre_in_q[1, 1], ("pre_in", 1, 1))
+        quantize_staged(pre_in_q[1, 2], ("pre_in", 1, 2))
+        turn_pre_in(2, 0)
+        turn_a(0, 0, "scalar")
+        weave_z("vector", 0, 0)
+        weave_z("vector", 0, 1)
+        product_a(2, 0)
+        quantize_z(0, 0)
+        quantize_z(0, 1)
+        quantize_staged(pre_in_q[2, 0], ("pre_in", 2, 0))
+        quantize_staged(a_q[0, 0], ("a", 0, 0))
         turn_pre_in(2, 1)
         turn_pre_in(2, 2)
+        product_z(1, range(4))
         quantize_staged(pre_in_q[2, 1], ("pre_in", 2, 1))
         quantize_staged(pre_in_q[2, 2], ("pre_in", 2, 2))
-        a_order = [(g, h) for h in range(2) for g in range(3)]
-        for g in range(3):
-            product_z(g, range(4))
-            first, second = a_order[2 * g], a_order[2 * g + 1]
-            turn_a(*first, "scalar")
-            weave_z("vector", g, 0)
-            turn_a(*second, "vector" if g < 2 else "scalar")
-            weave_z("vector", g, 1)
-            quantize_z(g, 0)
-            quantize_z(g, 1)
-            quantize_staged(a_q[first], ("a", *first))
-            quantize_staged(a_q[second], ("a", *second))
+        turn_a(0, 1, "scalar")
+        turn_a(1, 0, "scalar")
+        weave_z("vector", 1, 0)
+        weave_z("vector", 1, 1)
+        product_a(2, 1)
+        quantize_z(1, 0)
+        quantize_z(1, 1)
+        quantize_staged(a_q[0, 1], ("a", 0, 1))
+        quantize_staged(a_q[1, 0], ("a", 1, 0))
+        turn_a(1, 1, "scalar")
+        turn_a(2, 0, "scalar")
+        product_z(2, range(4))
+        quantize_staged(a_q[1, 1], ("a", 1, 1))
+        quantize_staged(a_q[2, 0], ("a", 2, 0))
+        turn_a(2, 1, "scalar")
+        weave_z("vector", 2, 0)
+        weave_z("vector", 2, 1)
+        quantize_z(2, 0)
+        quantize_z(2, 1)
+        quantize_staged(a_q[2, 1], ("a", 2, 1))
         for st in range(4):
             open_y(st, 0)
         for st in range(4):

from contextlib import ExitStack

import concourse.mybir as mybir
from concourse.masks import make_identity

T, D, F = 512, 1536, 1024
FLOPS = 2 * D * F * F + 2 * D * D * T + 2 * T * D * F

F32 = mybir.dt.float32
BF16 = mybir.dt.bfloat16
U32 = mybir.dt.uint32
I32 = mybir.dt.int32
U8 = mybir.dt.uint8
FP8X4 = mybir.dt.float8_e4m3fn_x4
MULT = mybir.AluOpType.mult
ADD = mybir.AluOpType.add
SUBTRACT = mybir.AluOpType.subtract
COPY = mybir.ActivationFunctionType.Copy

P = 128
PASS = 512
D_GROUPS = D // PASS
F_GROUPS = F // PASS
S_TILES = T // P
LOAD_SLOTS = 12
ALIGN = 64


def tile_preconditioned_momentum_outputs_h3_kernel(
    tc, mom, pre_out, damp, pre_in, lr, xt, base, out_0, out_1, out_2
):
    nc = tc.nc
    with ExitStack() as ctx:
        keep = ctx.enter_context(tc.tile_pool(name="keep", bufs=1))
        psum = ctx.enter_context(tc.psum_pool(name="psum", bufs=1))
        ctx.enter_context(tc.manual_schedule())

        taken = {}

        def rotating(pool, tag, slots, shape, dtype):
            turn = taken.get(tag, 0)
            taken[tag] = turn + 1
            name = "%s%d" % (tag, turn % slots)
            if pool == "psum":
                return psum.tile(shape, dtype, name=name, tag=name)
            return keep.tile(shape, dtype, name=name, tag=name, align_bytes=ALIGN)

        def operand(name):
            codes = keep.tile([P, PASS], U32, name=name + "_codes", align_bytes=ALIGN)
            scales = keep.tile([P, PASS], U8, name=name + "_scales", align_bytes=ALIGN)
            return codes, scales

        def quantize(q, grouped, c0=0, width=PASS):
            nc.vector.quantize_mx(
                out=q[0][:, c0 : c0 + width].bitcast(FP8X4),
                scales=q[1][:, c0 : c0 + width],
                in_=grouped,
            )

        def matmul(acc, stat, s0, mov, m0, width, start, stop):
            nc.tensor.matmul_mx(
                out=acc,
                lhsT=stat[0][:, s0 : s0 + P].bitcast(FP8X4),
                lhsT_scale=stat[1][:, s0 : s0 + P],
                rhs=mov[0][:, m0 : m0 + width].bitcast(FP8X4),
                rhs_scale=mov[1][:, m0 : m0 + width],
                start=start,
                stop=stop,
            )

        raw = {}

        def load(key, src, slot):
            raw[key] = keep.tile(list(src.shape), BF16, name="raw_" + slot, tag=slot, align_bytes=ALIGN)
            nc.sync.dma_start(out=raw[key][:], in_=src)

        def load_mom(g, u):
            rows = mom[PASS * g : PASS * (g + 1), :].rearrange("(m t) k -> m t k", t=4)
            load(("mom", g, u), rows[:, 2 * u : 2 * u + 2, :], "slot%d" % (2 * g + u))

        def load_pre_out(kk):
            rows = pre_out[PASS * kk : PASS * (kk + 1), :]
            load(("pre_out", kk), rows.rearrange("(p j) c -> p j c", j=4), "wide%d" % kk)

        def load_pre_in(g, v):
            rows = pre_in[PASS * g : PASS * (g + 1), :].rearrange("(m t) k -> m t k", t=4)
            slot = "wide%d" % v if g == D_GROUPS - 1 else "mid%d" % (2 * g + v)
            load(("pre_in", g, v), rows[:, 2 * v : 2 * v + 2, :], slot)

        def load_xt(kk):
            load(("xt", kk), xt[PASS * kk : PASS * (kk + 1), :].rearrange("(p j) s -> p j s", j=4), "slot%d" % kk)

        def load_base(i):
            load(("base", i), base[2 * P * i : 2 * P * (i + 1), :].rearrange("(a p) f -> p a f", p=P), "slot%d" % (3 + i))

        ident = keep.tile([P, P], F32, name="ident")
        damp_sb = keep.tile([P, F_GROUPS, 4], BF16, name="damp_sb")
        lr_sb = keep.tile([P, D_GROUPS, 4], BF16, name="lr_sb")
        lr_f = keep.tile([P, D_GROUPS, 4], F32, name="lr_f")
        mom_t = {}
        mom_q, pre_out_q, pre_in_q, xt_q, a_q, z_q = {}, {}, {}, {}, {}, {}
        for g in range(D_GROUPS):
            z_q[g] = operand("z%d" % g)
            xt_q[g] = operand("xt%d" % g)
            for kk in range(D_GROUPS):
                pre_in_q[g, kk] = operand("pre_in%d%d" % (g, kk))
            for h in range(F_GROUPS):
                mom_q[g, h] = operand("mom%d%d" % (g, h))
                a_q[g, h] = operand("a%d%d" % (g, h))
                mom_t[g, h] = keep.tile([P, PASS * 4], BF16, name="mom_t%d%d" % (g, h), tag="mom_t%d%d" % (g, h), align_bytes=ALIGN)
        for kk in range(F_GROUPS):
            for h in range(F_GROUPS):
                pre_out_q[kk, h] = operand("pre_out%d%d" % (kk, h))
        y_scales = keep.tile([P, F_GROUPS, T], U8, name="y_scales", align_bytes=ALIGN)
        grouped = {}

        def copy_on(engine, out, in_):
            if engine == "vector":
                nc.vector.tensor_copy(out=out, in_=in_)
            else:
                nc.scalar.copy(out=out, in_=in_)

        free_slots = list(range(6))
        slot_of = {}

        def stage(key):
            if key not in grouped:
                slot_of[key] = free_slots[0]
                free_slots.remove(slot_of[key])
                name = "grouped%d" % slot_of[key]
                grouped[key] = keep.tile([P, PASS * 4], BF16, name=name, tag=name, align_bytes=ALIGN)
            return grouped[key]

        def quantize_staged(q, key):
            quantize(q, grouped[key][:])
            free_slots.append(slot_of[key])

        def weave_pre_out(engine, kk, h, t0, t1):
            key = ("pre_out", kk, h)
            dst = stage(key)[:].rearrange("p (t m j) -> p t m j", t=4, j=4)
            src = raw["pre_out", kk][:, :, PASS * h : PASS * (h + 1)].rearrange("p j (m t) -> p t m j", t=4)
            copy_on(engine, dst[:, t0:t1], src[:, t0:t1])

        def weave_xt(engine, kk, q0, q1):
            key = ("xt", kk)
            dst = stage(key)[:].rearrange("p (c i j) -> p c j i", i=4, j=4)
            src = raw[key][:].rearrange("p j (c i) -> p c j i", i=4)
            copy_on(engine, dst[:, 32 * q0 : 32 * q1], src[:, 32 * q0 : 32 * q1])

        def turn_mom(g, u):
            words = raw["mom", g, u][:].bitcast(F32)
            for kk in range(F_GROUPS):
                bank = rotating("psum", "turn", 4, [P, 2, 2, P], F32)
                for e in range(2):
                    for w in range(2):
                        nc.tensor.transpose(bank[:, e, w, :], words[:, e, 256 * kk + w : 256 * (kk + 1) : 2], ident[:])
                dst = mom_t[g, kk][:].bitcast(F32).rearrange("p (u m e w) -> p u m e w", u=2, e=2, w=2)
                nc.scalar.copy(out=dst[:, u], in_=bank[:].rearrange("p e w m -> p m e w"))

        def turn_pre_in(g, kk):
            dst = stage(("pre_in", g, kk))[:].bitcast(F32).rearrange("p (t m w) -> p t m w", t=4, w=2)
            for v in range(2):
                words = raw["pre_in", g, v][:].bitcast(F32)
                bank = rotating("psum", "turn", 4, [P, 2, 2, P], F32)
                for e in range(2):
                    for w in range(2):
                        nc.tensor.transpose(bank[:, e, w, :], words[:, e, 256 * kk + w : 256 * (kk + 1) : 2], ident[:])
                nc.scalar.copy(out=dst[:, 2 * v : 2 * v + 2], in_=bank[:].rearrange("p e w m -> p e m w"))

        a_t = {}

        a_banks = {}

        def open_a(g, h):
            a_banks[g, h] = [rotating("psum", "acc", 4, [P, PASS], F32) for t in range(4)]
            for t in range(4):
                matmul(a_banks[g, h][t][:], pre_out_q[0, h], P * t, mom_q[g, 0], 0, PASS, True, False)

        def finish_a(g, h, t, bank):
            matmul(bank[:], pre_out_q[1, h], P * t, mom_q[g, 1], 0, PASS, False, True)
            if t == 0:
                a_t[g, h] = rotating("sbuf", "a_t", 6, [P, 4, PASS], BF16)
            nc.vector.scalar_tensor_tensor(
                out=a_t[g, h][:, t, :],
                in0=mom_t[g, h][:].rearrange("p (c t) -> p t c", t=4)[:, t, :],
                scalar=damp_sb[:, h, t : t + 1],
                in1=bank[:],
                op0=MULT,
                op1=ADD,
            )

        def close_a(g, h, slots):
            for t in slots:
                finish_a(g, h, t, a_banks[g, h][t])

        def product_a(g, h, slots=range(4)):
            for t in slots:
                bank = rotating("psum", "acc", 4, [P, PASS], F32)
                matmul(bank[:], pre_out_q[0, h], P * t, mom_q[g, 0], 0, PASS, True, False)
                finish_a(g, h, t, bank)

        def turn_a(g, h, last_bank):
            key = ("a", g, h)
            words = a_t[g, h][:].bitcast(F32)
            dst = stage(key)[:].bitcast(F32).rearrange("p (t m u) -> p t m u", t=4, u=2)
            for v in range(2):
                bank = rotating("psum", "turn", 4, [P, 2, 2, P], F32)
                for e in range(2):
                    for u in range(2):
                        nc.tensor.transpose(bank[:, e, u, :], words[:, 2 * v + e, P * u : P * (u + 1)], ident[:])
                copy_on(("scalar", last_bank)[v], dst[:, 2 * v : 2 * v + 2], bank[:].rearrange("p e u m -> p e m u"))

        z_b = {}

        def product_z(g, slots):
            for t in slots:
                if t == 0:
                    z_b[g] = keep.tile([P, 4, T], BF16, name="z_b%d" % g, tag="mom_t%d0" % g, align_bytes=ALIGN)
                bank = rotating("psum", "acc", 4, [P, T], F32)
                for kk in range(D_GROUPS):
                    matmul(bank[:], pre_in_q[g, kk], P * t, xt_q[kk], 0, T, kk == 0, kk == D_GROUPS - 1)
                nc.scalar.activation(out=z_b[g][:, t, :], in_=bank[:], func=COPY, scale=lr_f[:, g, t : t + 1])

        def weave_z(engine, g, half):
            dst = stage(("z", g))[:].rearrange("p (c i j) -> p c j i", i=4, j=4)
            src = z_b[g][:].rearrange("p j (c i) -> p c j i", i=4)
            copy_on(engine, dst[:, 64 * half : 64 * (half + 1)], src[:, 64 * half : 64 * (half + 1)])

        def quantize_z(g, half):
            quantize(z_q[g], grouped["z", g][:, 1024 * half : 1024 * (half + 1)], 256 * half, 256)
            if half == 1:
                free_slots.append(slot_of["z", g])

        y_b = {}

        y_banks, y_f = {}, {}

        def open_y(st, h):
            y_banks[st, h] = rotating("psum", "acc", 4, [P, PASS], F32)
            for g in range(D_GROUPS - 1):
                matmul(y_banks[st, h][:], z_q[g], P * st, a_q[g, h], 0, PASS, g == 0, False)

        def close_y(st, h, last=False):
            bank = y_banks[st, h]
            matmul(bank[:], z_q[D_GROUPS - 1], P * st, a_q[D_GROUPS - 1, h], 0, PASS, False, True)
            y = keep.tile([P, PASS], F32, name="y", tag=("mid%d", "slot%d")[h] % (st if st < 3 or h == 0 else 5), align_bytes=ALIGN)
            y_b[st, h] = rotating("sbuf", "y_b", 8, [P, PASS], BF16)
            sorted_b = y_b[st, h][:].rearrange("p (u m e) -> p u m e", u=2, e=2)
            cols = slice(PASS * h, PASS * (h + 1))
            base_sb = raw["base", st // 2][:, st % 2, cols]
            if last:
                nc.vector.tensor_tensor(
                    out=sorted_b,
                    in0=base_sb.rearrange("p (m u e) -> p u m e", u=2, e=2),
                    in1=bank[:].rearrange("p (u e m) -> p u m e", u=2, e=2),
                    op=SUBTRACT,
                )
            nc.vector.tensor_tensor(
                out=y[:].rearrange("p (m t) -> p m t", t=4),
                in0=base_sb.rearrange("p (m t) -> p m t", t=4),
                in1=bank[:].rearrange("p (t m) -> p m t", t=4),
                op=SUBTRACT,
            )
            nc.sync.dma_start(out=out_0[P * st : P * (st + 1), cols], in_=y[:])
            y_f[st, h] = y

        def round_y(st, h):
            nc.scalar.copy(
                out=y_b[st, h][:].rearrange("p (u m e) -> p u m e", u=2, e=2),
                in_=y_f[st, h][:].rearrange("p (m u e) -> p u m e", u=2, e=2),
            )

        y_g = {}

        def turn_y(h, tiles):
            n = len(tiles)
            bank = rotating("psum", "turn", 4, [P, n, 2, P], F32)
            for i, st in enumerate(tiles):
                words = y_b[st, h][:].bitcast(F32)
                for u in range(2):
                    nc.tensor.transpose(bank[:, i, u, :], words[:, P * u : P * (u + 1)], ident[:])
            y_g[h, tiles[0]] = rotating("sbuf", "y_g", 3, [P, n * P * 4], BF16)
            nc.scalar.copy(
                out=y_g[h, tiles[0]][:].bitcast(F32).rearrange("p (i s u) -> p i s u", i=n, u=2),
                in_=bank[:].rearrange("p i u s -> p i s u"),
            )

        def planes_y(h, tiles):
            cols = slice(P * tiles[0], P * (tiles[-1] + 1))
            codes = rotating("sbuf", "y_codes", 5, [P, len(tiles) * P], U32)
            quantize((codes, y_scales[:, h, cols]), y_g[h, tiles[0]][:], 0, len(tiles) * P)
            words = out_1[h].rearrange("p s b -> p (s b)").bitcast(I32)
            nc.sync.dma_start(out=words[:, cols], in_=codes[:].bitcast(I32))

        def store_scales():
            for q in range(4):
                queue = nc.scalar if q % 2 else nc.sync
                queue.dma_start(
                    out=out_2[:, 4 * q : 4 * q + 4, :].rearrange("h r s -> r h s").bitcast(I32),
                    in_=y_scales[32 * q : 32 * q + 4].bitcast(I32),
                )


        make_identity(nc, ident[:])
        load_mom(0, 0)
        load_mom(0, 1)
        load_pre_out(0)
        load_mom(1, 0)
        load_pre_out(1)
        with nc.allow_non_contiguous_dma(reason="one short run of a vector to each partition"):
            nc.sync.dma_start(out=damp_sb[:], in_=damp.rearrange("(h p t) -> p h t", p=P, t=4))
            nc.sync.dma_start(out=lr_sb[:], in_=lr.rearrange("(g p t) -> p g t", p=P, t=4))
        load_mom(1, 1)
        load_mom(2, 0)
        load_mom(2, 1)

        turn_mom(0, 0)
        turn_mom(0, 1)
        quantize(mom_q[0, 0], mom_t[0, 0][:])
        quantize(mom_q[0, 1], mom_t[0, 1][:])
        weave_pre_out("vector", 0, 0, 0, 2)
        weave_pre_out("scalar", 0, 0, 2, 4)
        quantize_staged(pre_out_q[0, 0], ("pre_out", 0, 0))
        turn_mom(1, 0)
        load_xt(0)
        load_pre_in(0, 0)
        load_pre_in(0, 1)
        load_xt(1)
        load_pre_in(1, 0)
        load_pre_in(1, 1)
        load_xt(2)
        weave_pre_out("vector", 0, 1, 0, 4)
        open_a(0, 0)
        weave_pre_out("vector", 1, 0, 0, 2)
        weave_pre_out("scalar", 1, 0, 2, 4)
        quantize_staged(pre_out_q[0, 1], ("pre_out", 0, 1))
        quantize_staged(pre_out_q[1, 0], ("pre_out", 1, 0))
        weave_pre_out("scalar", 1, 1, 0, 2)
        weave_pre_out("vector", 1, 1, 2, 4)
        turn_mom(1, 1)
        nc.scalar.copy(out=lr_f[:], in_=lr_sb[:])
        quantize_staged(pre_out_q[1, 1], ("pre_out", 1, 1))
        close_a(0, 0, range(4))
        turn_mom(2, 0)
        turn_mom(2, 1)
        load_pre_in(2, 0)
        load_pre_in(2, 1)
        load_base(0)
        load_base(1)
        quantize(mom_q[1, 0], mom_t[1, 0][:])
        quantize(mom_q[1, 1], mom_t[1, 1][:])
        weave_xt("scalar", 0, 0, 4)
        product_a(0, 1)
        turn_pre_in(0, 0)
        turn_pre_in(0, 1)
        quantize_staged(xt_q[0], ("xt", 0))
        quantize_staged(pre_in_q[0, 0], ("pre_in", 0, 0))
        quantize_staged(pre_in_q[0, 1], ("pre_in", 0, 1))
        weave_xt("scalar", 1, 0, 4)
        product_a(1, 0)
        turn_pre_in(0, 2)
        turn_pre_in(1, 0)
        quantize_staged(xt_q[1], ("xt", 1))
        quantize_staged(pre_in_q[0, 2], ("pre_in", 0, 2))
        quantize_staged(pre_in_q[1, 0], ("pre_in", 1, 0))
        weave_xt("scalar", 2, 0, 4)
        product_a(1, 1, range(2))
        quantize_staged(xt_q[2], ("xt", 2))
        product_a(1, 1, range(2, 4))
        turn_pre_in(1, 1)
        turn_pre_in(1, 2)
        quantize(mom_q[2, 0], mom_t[2, 0][:])
        quantize(mom_q[2, 1], mom_t[2, 1][:])
        product_z(0, range(4))
        quantize_staged(pre_in_q[1, 1], ("pre_in", 1, 1))
        quantize_staged(pre_in_q[1, 2], ("pre_in", 1, 2))
        turn_pre_in(2, 0)
        turn_a(0, 0, "scalar")
        weave_z("vector", 0, 0)
        weave_z("vector", 0, 1)
        product_a(2, 0)
        quantize_z(0, 0)
        quantize_z(0, 1)
        quantize_staged(pre_in_q[2, 0], ("pre_in", 2, 0))
        quantize_staged(a_q[0, 0], ("a", 0, 0))
        turn_pre_in(2, 1)
        turn_pre_in(2, 2)
        product_z(1, range(4))
        quantize_staged(pre_in_q[2, 1], ("pre_in", 2, 1))
        quantize_staged(pre_in_q[2, 2], ("pre_in", 2, 2))
        turn_a(0, 1, "scalar")
        turn_a(1, 0, "scalar")
        weave_z("vector", 1, 0)
        weave_z("vector", 1, 1)
        product_a(2, 1)
        quantize_z(1, 0)
        quantize_z(1, 1)
        quantize_staged(a_q[0, 1], ("a", 0, 1))
        quantize_staged(a_q[1, 0], ("a", 1, 0))
        turn_a(1, 1, "scalar")
        turn_a(2, 0, "scalar")
        product_z(2, range(4))
        quantize_staged(a_q[1, 1], ("a", 1, 1))
        quantize_staged(a_q[2, 0], ("a", 2, 0))
        turn_a(2, 1, "scalar")
        weave_z("vector", 2, 0)
        weave_z("vector", 2, 1)
        quantize_z(2, 0)
        quantize_z(2, 1)
        quantize_staged(a_q[2, 1], ("a", 2, 1))
        for st in range(4):
            open_y(st, 0)
        for st in range(4):
            close_y(st, 0)
            round_y(st, 0)
        for st in range(2):
            open_y(st, 1)
            close_y(st, 1)
        turn_y(0, [0, 1])
        turn_y(0, [2, 3])
        round_y(0, 1)
        round_y(1, 1)
        planes_y(0, [0, 1])
        planes_y(0, [2, 3])
        open_y(2, 1)
        close_y(2, 1)
        round_y(2, 1)
        open_y(3, 1)
        close_y(3, 1, last=True)
        turn_y(1, [0, 1])
        turn_y(1, [2])
        turn_y(1, [3])
        planes_y(1, [0, 1])
        planes_y(1, [2])
        planes_y(1, [3])
        store_scales()
